import numpy as np
import ml_dtypes


def mxq(x, axis, fmt="e4m3"):
    dtype, down = {"e4m3": (ml_dtypes.float8_e4m3fn, 7), "e5m2": (ml_dtypes.float8_e5m2, 14)}[fmt]
    v = np.moveaxis(np.asarray(x, np.float32).astype(ml_dtypes.bfloat16).astype(np.float64), axis, -1)
    blocks = v.reshape(v.shape[:-1] + (-1, 32))
    amax = np.abs(blocks).max(-1, keepdims=True)
    byte = np.maximum(np.where(amax > 0, np.frexp(amax)[1] - 1 + 127, 0) - down, 1)
    scale = np.exp2(byte - 127.0)
    codes = (blocks / scale).astype(np.float32).astype(dtype).astype(np.float64)
    return np.moveaxis((codes * scale).reshape(v.shape), -1, axis)


WIDE = False


def mx_kscale(k):
    if not WIDE:
        return np.ones(k)
    levels = np.array([30, -30])
    if k % 512:
        return np.exp2(np.random.permutation(np.resize(levels, k // 32))).repeat(32)
    a = np.empty((k // 512, 16))
    for p in range(k // 512):
        a[p, :8] = np.random.permutation(np.resize(levels, 8))
        for g in range(8):
            far = levels[np.abs(levels - a[p, g]) >= 10]
            a[p, g + 8] = far[np.random.randint(len(far))]
    return np.exp2(a.ravel()).repeat(32)


def f64(x):
    return np.asarray(x).astype(np.float64)


def striped(idx):
    return np.tile(np.asarray(idx).reshape(-1, 16).T, (8, 1)).astype(np.uint16)


def unstriped(offs):
    return offs[:16].T.reshape(-1).astype(np.int64)


E2M1 = np.array([0.0, 0.5, 1.0, 1.5, 2.0, 3.0, 4.0, 6.0, -0.0, -0.5, -1.0, -1.5, -2.0, -3.0, -4.0, -6.0])


def pack_weight(w, fmt):
    k, n = w.shape
    w = f64(np.asarray(w, np.float32).astype(ml_dtypes.bfloat16)).reshape(k // 32, 32, n)
    amax = np.abs(w).max(1)
    if fmt in ("e4m3", "e5m2"):
        byte = np.frexp(amax)[1] - 1 + 127 - (7 if fmt == "e4m3" else 14)
    else:
        mant, ex = np.frexp(amax / 6.0)
        byte = np.where(mant > 0.5, ex, ex - 1) + 127
    byte = np.clip(np.where(amax > 0, byte, 1), 1, 254)
    scaled = (w * np.exp2(127.0 - byte)[:, None, :]).reshape(k, n).astype(np.float32)
    by_word = np.ascontiguousarray(scaled.reshape(k // 512, 128, 4, n).transpose(0, 1, 3, 2))
    if fmt in ("e4m3", "e5m2"):
        words = by_word.astype(ml_dtypes.float8_e4m3fn if fmt == "e4m3" else ml_dtypes.float8_e5m2).view(np.uint8)
    else:
        c = by_word.astype(ml_dtypes.float4_e2m1fn).view(np.uint8) & 0xF
        words = (c[..., 0::2] | (c[..., 1::2] << 4)).reshape(k // 512, 128, 2 * n)
    return np.ascontiguousarray(words), np.ascontiguousarray(byte.astype(np.uint8).reshape(k // 512, 16, n))


def unpack_weight(words, scales, fmt):
    g, _, n = scales.shape
    words = np.ascontiguousarray(words).reshape(g, 128, n, -1)
    if fmt in ("e4m3", "e5m2"):
        vals = words.view(ml_dtypes.float8_e4m3fn if fmt == "e4m3" else ml_dtypes.float8_e5m2).astype(np.float64)
    else:
        nib = np.empty((g, 128, n, 4), np.uint8)
        nib[..., 0::2] = words & 0xF
        nib[..., 1::2] = words >> 4
        vals = E2M1[nib]
    vals = vals * np.repeat(np.exp2(scales.astype(np.float64) - 127.0), 8, axis=1)[..., None]
    return vals.transpose(0, 1, 3, 2).reshape(g * 512, n)


K, T, J, R, F, Z, C, X, O, N, U = 512, 1024, 256, 512, 512, 1024, 512, 1024, 256, 256, 128


def setup_inputs():
    n = np.random.standard_normal
    idx = np.random.permutation(T)[:J]
    idx2 = np.random.permutation(Z)[:J]
    idx3 = np.random.permutation(C)[:J]
    idx4 = np.random.permutation(X)[:C]
    idx5 = np.random.permutation(C)[:O]
    idx6 = np.random.permutation(O)[:U]
    idx7 = np.random.permutation(O)[:U]
    fk = mx_kscale(K)
    ff = mx_kscale(F)
    fr = mx_kscale(R)
    xtp = pack_weight(n((K, T)) / fk[:, None], "e2m1")
    xop = pack_weight(n((F, Z)) / ff[:, None], "e5m2")
    wp = pack_weight(n((K, R)) * 1 / np.sqrt(K) * fk[:, None] * fr, "e5m2")
    w0p = pack_weight(n((F, R)) * 1 / np.sqrt(F) * ff[:, None] * fr, "e4m3")
    wbp = pack_weight(n((R, N)) * 1 / np.sqrt(R) / fr[:, None], "e4m3")
    return {
        "xt_words": xtp[0],
        "xt_scales": xtp[1],
        "xo_words": xop[0],
        "xo_scales": xop[1],
        "w_words": wp[0],
        "w_scales": wp[1],
        "w0_words": w0p[0],
        "w0_scales": w0p[1],
        "tb": (n((R, X)) * 0.9).astype(np.float32),
        "wb_words": wbp[0],
        "wb_scales": wbp[1],
        "so": (np.random.uniform(0.5, 1.6, (N, 1))).astype(np.float32),
        "sp": (np.random.uniform(0.5, 1.6, (N, 1))).astype(np.float32),
        "offs": striped(idx),
        "offs2": striped(idx2),
        "offs3": striped(idx3),
        "offs4": striped(idx4),
        "offs5": striped(idx5),
        "offs6": striped(idx6),
        "offs7": striped(idx7),
    }


def reference(xt_words, xt_scales, xo_words, xo_scales, w_words, w_scales, w0_words, w0_scales, tb, wb_words, wb_scales, so, sp, offs, offs2, offs3, offs4, offs5, offs6, offs7):
    idx = unstriped(offs)
    idx2 = unstriped(offs2)
    idx3 = unstriped(offs3)
    idx4 = unstriped(offs4)
    idx5 = unstriped(offs5)
    idx6 = unstriped(offs6)
    idx7 = unstriped(offs7)
    xtu = unpack_weight(xt_words, xt_scales, "e2m1")
    xou = unpack_weight(xo_words, xo_scales, "e5m2")
    wu = unpack_weight(w_words, w_scales, "e5m2")
    w0u = unpack_weight(w0_words, w0_scales, "e4m3")
    wbu = unpack_weight(wb_words, wb_scales, "e4m3")
    xtidxg = xtu[:, idx]
    xoidx2g = xou[:, idx2]
    a = wu.T @ xtidxg + w0u.T @ xoidx2g
    la = a[:, 0:1]
    pw = np.zeros((R, C))
    pw[:, idx3] = a
    pg = np.abs(pw - f64(tb)[:, idx4] * la)
    hid = pg[:, idx5]
    hidq = mxq(hid, 0, "e5m2")
    p = wbu.T @ hidq
    y = np.maximum(p[:, idx6] * f64(so), p[:, idx7] * f64(sp))
    return y

@@ -1,0 +1,206 @@
+from contextlib import ExitStack
+
+import concourse.mybir as mybir
+
+K, T, J, R, F, Z, C, X, O, N, U = 512, 1024, 256, 512, 512, 1024, 512, 1024, 256, 256, 128
+FLOPS = 2 * K * R * J + 2 * F * R * J + 2 * R * N * O
+
+F32 = mybir.dt.float32
+BF16 = mybir.dt.bfloat16
+I32 = mybir.dt.int32
+U32 = mybir.dt.uint32
+U16 = mybir.dt.uint16
+U8 = mybir.dt.uint8
+E4M3 = mybir.dt.float8_e4m3fn_x4
+E5M2 = mybir.dt.float8_e5m2_x4
+E2M1 = mybir.dt.float4_e2m1fn_x4
+ACT = mybir.ActivationFunctionType
+ALU = mybir.AluOpType
+
+P = 128
+PACK = 4
+QUADS = 4
+
+
+def tile_list_stamplead_bank_one_pairweighed_kernel(
+    tc, xt_words, xt_scales, xo_words, xo_scales, w_words, w_scales, w0_words, w0_scales, tb,
+    wb_words, wb_scales, so, sp, offs, offs2, offs3, offs4, offs5, offs6, offs7, out,
+):
+    nc = tc.nc
+    with ExitStack() as ctx:
+        sb = ctx.enter_context(tc.tile_pool(name="sb", bufs=1))
+        ps = ctx.enter_context(tc.psum_pool(name="ps", bufs=1))
+
+        def load_list(src, name):
+            tile = sb.tile(list(src.shape), U16, name=name)
+            nc.sync.dma_start(tile[:], src)
+            return tile
+
+        def load_words(src, name):
+            tile = sb.tile([P, src.shape[2]], U32, name=name, align_bytes=64)
+            nc.sync.dma_start(tile[:].bitcast(I32), src[0].rearrange("p n t -> p (n t)").bitcast(I32))
+            return tile
+
+        def zeroed_plane(width, name):
+            tile = sb.tile([P, width], U8, name=name, align_bytes=64)
+            nc.vector.memset(tile[:].bitcast(I32), 0)
+            return tile
+
+        def load_plane(tile, src):
+            for q in range(QUADS):
+                nc.sync.dma_start(tile[32 * q : 32 * q + 4, :].bitcast(I32), src[0, 4 * q : 4 * q + 4, :].bitcast(I32))
+
+        xo_plane = zeroed_plane(Z, "xo_plane")
+        xt_plane = zeroed_plane(T, "xt_plane")
+        ww_plane = zeroed_plane(2 * R, "ww_plane")
+        wb_plane = zeroed_plane(N, "wb_plane")
+        pw = [sb.tile([P, C], F32, name="pw%d" % t) for t in range(PACK)]
+
+        ww_stage = sb.tile([4, QUADS, 2 * R // 4], I32, name="ww_stage")
+        for i, src in enumerate((w0_scales, w_scales)):
+            nc.sync.dma_start(
+                ww_stage[:, :, i * R // 4 : (i + 1) * R // 4],
+                src[0].bitcast(I32).rearrange("(q r) c -> r q c", r=4),
+            )
+        l2 = load_list(offs2, "l2")
+        xo_w = load_words(xo_words, "xo_w")
+        load_plane(xo_plane, xo_scales)
+        w0_w = load_words(w0_words, "w0_w")
+        xt_w = sb.tile([P, T], U16, name="xt_w")
+        nc.sync.dma_start(xt_w[:].bitcast(I32), xt_words[0].bitcast(I32))
+        l1 = load_list(offs, "l1")
+        w_w = load_words(w_words, "w_w")
+        load_plane(xt_plane, xt_scales)
+        tb_rows = tb.rearrange("(p t) x -> p t x", t=PACK)
+        tbs = [sb.tile([P, X], F32, name="tb%d" % t, tag="tb%d" % t) for t in range(PACK)]
+        nc.sync.dma_start(tbs[0][:], tb_rows[:, 0, :])
+        l4 = load_list(offs4, "l4")
+        l3 = load_list(offs3, "l3")
+        for t in range(1, PACK):
+            nc.sync.dma_start(tbs[t][:], tb_rows[:, t, :])
+        l5 = load_list(offs5, "l5")
+        wb_w = load_words(wb_words, "wb_w")
+        load_plane(wb_plane, wb_scales)
+        l6 = load_list(offs6, "l6")
+        l7 = load_list(offs7, "l7")
+        so_sb = sb.tile([P, N // P], F32, name="so_sb")
+        sp_sb = sb.tile([P, N // P], F32, name="sp_sb")
+        with nc.allow_non_contiguous_dma(reason="one weight a partition and half"):
+            nc.sync.dma_start(so_sb[:], so.rearrange("(h p) o -> p (h o)", p=P))
+            nc.sync.dma_start(sp_sb[:], sp.rearrange("(h p) o -> p (h o)", p=P))
+
+        ww_words = ww_plane[:].bitcast(I32)
+        for q in range(QUADS):
+            nc.vector.tensor_copy(ww_words[32 * q : 32 * q + 4, :], ww_stage[:, q, :])
+        ww_dealt = sb.tile([P, 2, PACK, P], U8, name="ww_dealt", align_bytes=64)
+        nc.vector.tensor_copy(ww_dealt[:], ww_plane[:].rearrange("p (i m t) -> p i t m", i=2, t=PACK))
+        w0_dealt = sb.tile([P, R], U32, name="w0_dealt", align_bytes=64)
+        w_dealt = sb.tile([P, R], U32, name="w_dealt", align_bytes=64)
+        for dealt, words in ((w0_dealt, w0_w), (w_dealt, w_w)):
+            nc.scalar.copy(
+                dealt[:].rearrange("p (t m) -> p m t", t=PACK), words[:].rearrange("p (m t) -> p m t", t=PACK)
+            )
+
+        xo_g = sb.tile([P, J], U32, name="xo_g", align_bytes=64)
+        xo_gs = sb.tile([P, J], U8, name="xo_gs", align_bytes=64)
+        xt_g = sb.tile([P, J], U16, name="xt_g", align_bytes=64)
+        xt_gs = sb.tile([P, J], U8, name="xt_gs", align_bytes=64)
+        nc.vector.tensor_copy(xo_gs[:], xo_plane[:].indirect(l2[:]))
+        nc.vector.tensor_copy(xo_g[:], xo_w[:].indirect(l2[:]))
+        nc.vector.tensor_copy(xt_g[:], xt_w[:].indirect(l1[:]))
+        nc.vector.tensor_copy(xt_gs[:], xt_plane[:].indirect(l1[:]))
+
+        for t in range(PACK):
+            nc.vector.memset(pw[t][:], 0.0)
+
+        a_ps = [ps.tile([P, J], F32, name="a_ps%d" % t) for t in range(PACK)]
+        for t in range(PACK):
+            nc.tensor.matmul_mx(
+                out=a_ps[t][:], lhsT=w0_dealt[:, t * P : (t + 1) * P].bitcast(E4M3), lhsT_scale=ww_dealt[:, 0, t, :],
+                rhs=xo_g[:].bitcast(E5M2), rhs_scale=xo_gs[:], start=True, stop=False,
+            )
+        for t in range(PACK):
+            nc.tensor.matmul_mx(
+                out=a_ps[t][:], lhsT=w_dealt[:, t * P : (t + 1) * P].bitcast(E5M2), lhsT_scale=ww_dealt[:, 1, t, :],
+                rhs=xt_g[:].bitcast(E2M1), rhs_scale=xt_gs[:], start=False, stop=True,
+            )
+
+        a_sb = [sb.tile([P, J], F32, name="a_sb%d" % t) for t in range(PACK)]
+        fetched = [sb.tile([P, C], F32, name="fetched%d" % t) for t in range(PACK)]
+        diff = [sb.tile([P, C], F32, name="diff%d" % t, tag="diff%d" % t) for t in range(PACK)]
+        pg = {}
+        hid_rows = sb.tile([P, PACK, O], BF16, name="hid_rows")
+        hid = sb.tile([P, O, PACK], BF16, name="hid", align_bytes=64)
+
+        def empty(t):
+            nc.vector.tensor_copy(a_sb[t][:], a_ps[t][:])
+
+        def fetch(t):
+            nc.scalar.activation(fetched[t][:], tbs[t][:].indirect(l4[:]), ACT.Copy, scale=a_sb[t][:, 0:1])
+
+        def place_v(t):
+            nc.vector.tensor_copy(pw[t][:].indirect(l3[:]), a_sb[t][:])
+
+        def place_s(t):
+            nc.scalar.activation(pw[t][:].indirect(l3[:]), a_sb[t][:], ACT.Copy)
+
+        def sub(t):
+            nc.vector.tensor_tensor(diff[t][:], pw[t][:], fetched[t][:], ALU.subtract)
+
+        def mag(t):
+            pg[t] = sb.tile([P, C], F32, name="pg%d" % t, tag="tb3" if t == 0 else "diff%d" % (t - 1))
+            nc.scalar.activation(pg[t][:], diff[t][:], ACT.Abs)
+
+        def pick_v(t):
+            nc.vector.tensor_copy(hid_rows[:, t, :], pg[t][:].indirect(l5[:]))
+
+        def pick_s(t):
+            nc.scalar.activation(hid_rows[:, t, :], pg[t][:].indirect(l5[:]), ACT.Copy)
+
+        def weave(t0):
+            nc.vector.tensor_copy(hid[:, :, t0 : t0 + 2], hid_rows[:, t0 : t0 + 2, :].rearrange("p t o -> p o t"))
+
+        for t in range(PACK):
+            empty(t)
+        fetch(0)
+        place_v(0)
+        fetch(1)
+        place_v(1)
+        place_s(3)
+        sub(0)
+        fetch(2)
+        place_v(2)
+        fetch(3)
+        sub(1)
+        mag(0)
+        pick_s(0)
+        sub(2)
+        mag(1)
+        sub(3)
+        mag(2)
+        pick_v(1)
+        mag(3)
+        pick_v(2)
+        pick_s(3)
+        weave(0)
+        weave(2)
+
+        hid_q = sb.tile([P, O], U32, name="hid_q", align_bytes=64)
+        hid_s = sb.tile([P, O], U8, name="hid_s", align_bytes=64)
+        nc.vector.quantize_mx(out=hid_q[:].bitcast(E5M2), scales=hid_s[:], in_=hid[:].rearrange("p o t -> p (o t)"))
+
+        for h in range(N // P):
+            p_ps = ps.tile([P, O], F32, name="p_ps%d" % h)
+            nc.tensor.matmul_mx(
+                out=p_ps[:], lhsT=wb_w[:, h * P : (h + 1) * P].bitcast(E4M3), lhsT_scale=wb_plane[:, h * P : (h + 1) * P],
+                rhs=hid_q[:].bitcast(E5M2), rhs_scale=hid_s[:], start=True, stop=True,
+            )
+            p_sb = sb.tile([P, O], F32, name="p_sb%d" % h)
+            nc.vector.tensor_copy(p_sb[:], p_ps[:])
+            first = sb.tile([P, U], F32, name="first%d" % h)
+            second = sb.tile([P, U], F32, name="second%d" % h)
+            nc.scalar.activation(first[:], p_sb[:].indirect(l6[:]), ACT.Copy, scale=so_sb[:, h : h + 1])
+            nc.scalar.activation(second[:], p_sb[:].indirect(l7[:]), ACT.Copy, scale=sp_sb[:, h : h + 1])
+            y = sb.tile([P, U], F32, name="y%d" % h)
+            nc.vector.tensor_tensor(y[:], first[:], second[:], ALU.max)
+            nc.sync.dma_start(out[h * P : (h + 1) * P, :], y[:])

@@ -135,6 +135,12 @@ def tile_list_stamplead_bank_one_pairweighed_kernel(
         def empty(t):
             nc.vector.tensor_copy(a_sb[t][:], a_ps[t][:])
 
+        def empty_s(t):
+            nc.scalar.copy(a_sb[t][:], a_ps[t][:])
+
+        def sub_g(t):
+            nc.gpsimd.tensor_tensor(diff[t][:], pw[t][:], fetched[t][:], ALU.subtract)
+
         def fetch(t):
             nc.scalar.activation(fetched[t][:], tbs[t][:].indirect(l4[:]), ACT.Copy, scale=a_sb[t][:, 0:1])
 
@@ -151,6 +157,10 @@ def tile_list_stamplead_bank_one_pairweighed_kernel(
             pg[t] = sb.tile([P, C], F32, name="pg%d" % t, tag="tb3" if t == 0 else "diff%d" % (t - 1))
             nc.scalar.activation(pg[t][:], diff[t][:], ACT.Abs)
 
+        def mag_v(t):
+            pg[t] = sb.tile([P, C], F32, name="pg%d" % t)
+            nc.vector.scalar_tensor_tensor(pg[t][:], diff[t][:], -1.0, diff[t][:], ALU.mult, ALU.max)
+
         def pick_v(t):
             nc.vector.tensor_copy(hid_rows[:, t, :], pg[t][:].indirect(l5[:]))
 
@@ -160,43 +170,59 @@ def tile_list_stamplead_bank_one_pairweighed_kernel(
         def weave(t0):
             nc.vector.tensor_copy(hid[:, :, t0 : t0 + 2], hid_rows[:, t0 : t0 + 2, :].rearrange("p t o -> p o t"))
 
-        for t in range(PACK):
-            empty(t)
+        empty(0)
+        empty_s(1)
         fetch(0)
         place_v(0)
+        empty_s(2)
+        sub_g(0)
         fetch(1)
         place_v(1)
-        place_s(3)
-        sub(0)
+        empty_s(3)
+        sub_g(1)
         fetch(2)
         place_v(2)
+        sub_g(2)
         fetch(3)
-        sub(1)
-        mag(0)
-        pick_s(0)
-        sub(2)
-        mag(1)
+        place_v(3)
         sub(3)
-        mag(2)
+        for t in range(PACK):
+            mag(t)
+        pick_v(0)
         pick_v(1)
-        mag(3)
-        pick_v(2)
-        pick_s(3)
+        pick_s(2)
         weave(0)
-        weave(2)
-
+        H = O // 2
+        nc.scalar.activation(hid_rows[:, 3, 0:H], pg[3][:].indirect(l5[:, 0 : H // 16]), ACT.Copy)
+        nc.vector.tensor_copy(hid_rows[:, 3, H:O], pg[3][:].indirect(l5[:, H // 16 : O // 16]))
         hid_q = sb.tile([P, O], U32, name="hid_q", align_bytes=64)
         hid_s = sb.tile([P, O], U8, name="hid_s", align_bytes=64)
-        nc.vector.quantize_mx(out=hid_q[:].bitcast(E5M2), scales=hid_s[:], in_=hid[:].rearrange("p o t -> p (o t)"))
+        for j in range(2):
+            nc.vector.tensor_copy(
+                hid[:, j * H : (j + 1) * H, 2:4], hid_rows[:, 2:4, j * H : (j + 1) * H].rearrange("p t o -> p o t")
+            )
+        for j in range(2):
+            nc.vector.quantize_mx(
+                out=hid_q[:, j * H : (j + 1) * H].bitcast(E5M2), scales=hid_s[:, j * H : (j + 1) * H],
+                in_=hid[:, j * H : (j + 1) * H, :].rearrange("p o t -> p (o t)"),
+            )
+        p_sbs = [sb.tile([P, O], F32, name="p_sb%d" % h) for h in range(N // P)]
+        for j in range(2):
+            for h in range(N // P):
+                p_ps = ps.tile([P, H], F32, name="p_ps%d_%d" % (h, j))
+                nc.tensor.matmul_mx(
+                    out=p_ps[:], lhsT=wb_w[:, h * P : (h + 1) * P].bitcast(E4M3),
+                    lhsT_scale=wb_plane[:, h * P : (h + 1) * P],
+                    rhs=hid_q[:, j * H : (j + 1) * H].bitcast(E5M2), rhs_scale=hid_s[:, j * H : (j + 1) * H],
+                    start=True, stop=True,
+                )
+                if j == 0:
+                    nc.scalar.copy(p_sbs[h][:, j * H : (j + 1) * H], p_ps[:])
+                else:
+                    nc.vector.tensor_copy(p_sbs[h][:, j * H : (j + 1) * H], p_ps[:])
 
         for h in range(N // P):
-            p_ps = ps.tile([P, O], F32, name="p_ps%d" % h)
-            nc.tensor.matmul_mx(
-                out=p_ps[:], lhsT=wb_w[:, h * P : (h + 1) * P].bitcast(E4M3), lhsT_scale=wb_plane[:, h * P : (h + 1) * P],
-                rhs=hid_q[:].bitcast(E5M2), rhs_scale=hid_s[:], start=True, stop=True,
-            )
-            p_sb = sb.tile([P, O], F32, name="p_sb%d" % h)
-            nc.vector.tensor_copy(p_sb[:], p_ps[:])
+            p_sb = p_sbs[h]
             first = sb.tile([P, U], F32, name="first%d" % h)
             second = sb.tile([P, U], F32, name="second%d" % h)
             nc.scalar.activation(first[:], p_sb[:].indirect(l6[:]), ACT.Copy, scale=so_sb[:, h : h + 1])

@@ -29,6 +29,7 @@ def tile_list_stamplead_bank_one_pairweighed_kernel(
     nc = tc.nc
     with ExitStack() as ctx:
         sb = ctx.enter_context(tc.tile_pool(name="sb", bufs=1))
+        table = ctx.enter_context(tc.tile_pool(name="table", bufs=1))
         ps = ctx.enter_context(tc.psum_pool(name="ps", bufs=1))
 
         def load_list(src, name):
@@ -62,21 +63,20 @@ def tile_list_stamplead_bank_one_pairweighed_kernel(
                 ww_stage[:, :, i * R // 4 : (i + 1) * R // 4],
                 src[0].bitcast(I32).rearrange("(q r) c -> r q c", r=4),
             )
+        load_plane(xo_plane, xo_scales)
         l2 = load_list(offs2, "l2")
         xo_w = load_words(xo_words, "xo_w")
-        load_plane(xo_plane, xo_scales)
+        l1 = load_list(offs, "l1")
+        load_plane(xt_plane, xt_scales)
         w0_w = load_words(w0_words, "w0_w")
         xt_w = sb.tile([P, T], U16, name="xt_w")
         nc.sync.dma_start(xt_w[:].bitcast(I32), xt_words[0].bitcast(I32))
-        l1 = load_list(offs, "l1")
         w_w = load_words(w_words, "w_w")
-        load_plane(xt_plane, xt_scales)
         tb_rows = tb.rearrange("(p t) x -> p t x", t=PACK)
-        tbs = [sb.tile([P, X], F32, name="tb%d" % t, tag="tb%d" % t) for t in range(PACK)]
-        nc.sync.dma_start(tbs[0][:], tb_rows[:, 0, :])
-        l4 = load_list(offs4, "l4")
+        tbs = [table.tile([P, X], F32, name="tb%d" % t, offset=t * X * 4) for t in range(PACK)]
         l3 = load_list(offs3, "l3")
-        for t in range(1, PACK):
+        l4 = load_list(offs4, "l4")
+        for t in range(PACK):
             nc.sync.dma_start(tbs[t][:], tb_rows[:, t, :])
         l5 = load_list(offs5, "l5")
         wb_w = load_words(wb_words, "wb_w")
@@ -96,9 +96,10 @@ def tile_list_stamplead_bank_one_pairweighed_kernel(
         nc.vector.tensor_copy(ww_dealt[:], ww_plane[:].rearrange("p (i m t) -> p i t m", i=2, t=PACK))
         w0_dealt = sb.tile([P, R], U32, name="w0_dealt", align_bytes=64)
         w_dealt = sb.tile([P, R], U32, name="w_dealt", align_bytes=64)
-        for dealt, words in ((w0_dealt, w0_w), (w_dealt, w_w)):
+        for dealt, words, lo, hi in ((w0_dealt, w0_w, 0, PACK), (w_dealt, w_w, 0, 1), (w_dealt, w_w, 1, PACK)):
             nc.scalar.copy(
-                dealt[:].rearrange("p (t m) -> p m t", t=PACK), words[:].rearrange("p (m t) -> p m t", t=PACK)
+                dealt[:].rearrange("p (t m) -> p m t", t=PACK)[:, :, lo:hi],
+                words[:].rearrange("p (m t) -> p m t", t=PACK)[:, :, lo:hi],
             )
 
         xo_g = sb.tile([P, J], U32, name="xo_g", align_bytes=64)
@@ -107,8 +108,8 @@ def tile_list_stamplead_bank_one_pairweighed_kernel(
         xt_gs = sb.tile([P, J], U8, name="xt_gs", align_bytes=64)
         nc.vector.tensor_copy(xo_gs[:], xo_plane[:].indirect(l2[:]))
         nc.vector.tensor_copy(xo_g[:], xo_w[:].indirect(l2[:]))
-        nc.vector.tensor_copy(xt_g[:], xt_w[:].indirect(l1[:]))
         nc.vector.tensor_copy(xt_gs[:], xt_plane[:].indirect(l1[:]))
+        nc.vector.tensor_copy(xt_g[:], xt_w[:].indirect(l1[:]))
 
         for t in range(PACK):
             nc.vector.memset(pw[t][:], 0.0)
@@ -154,7 +155,10 @@ def tile_list_stamplead_bank_one_pairweighed_kernel(
             nc.vector.tensor_tensor(diff[t][:], pw[t][:], fetched[t][:], ALU.subtract)
 
         def mag(t):
-            pg[t] = sb.tile([P, C], F32, name="pg%d" % t, tag="tb3" if t == 0 else "diff%d" % (t - 1))
+            if t == PACK - 1:
+                pg[t] = sb.tile([P, C], F32, name="pg%d" % t)
+            else:
+                pg[t] = table.tile([P, C], F32, name="pg%d" % t, offset=(2 * X * 4, 3 * X * 4, 3 * X * 4 + C * 4)[t])
             nc.scalar.activation(pg[t][:], diff[t][:], ACT.Abs)
 
         def mag_v(t):
@@ -171,7 +175,7 @@ def tile_list_stamplead_bank_one_pairweighed_kernel(
             nc.vector.tensor_copy(hid[:, :, t0 : t0 + 2], hid_rows[:, t0 : t0 + 2, :].rearrange("p t o -> p o t"))
 
         empty(0)
-        empty_s(1)
+        empty(1)
         fetch(0)
         place_v(0)
         empty_s(2)

from contextlib import ExitStack

import concourse.mybir as mybir

K, T, J, R, F, Z, C, X, O, N, U = 512, 1024, 256, 512, 512, 1024, 512, 1024, 256, 256, 128
FLOPS = 2 * K * R * J + 2 * F * R * J + 2 * R * N * O

F32 = mybir.dt.float32
BF16 = mybir.dt.bfloat16
I32 = mybir.dt.int32
U32 = mybir.dt.uint32
U16 = mybir.dt.uint16
U8 = mybir.dt.uint8
E4M3 = mybir.dt.float8_e4m3fn_x4
E5M2 = mybir.dt.float8_e5m2_x4
E2M1 = mybir.dt.float4_e2m1fn_x4
ACT = mybir.ActivationFunctionType
ALU = mybir.AluOpType

P = 128
PACK = 4
QUADS = 4


def tile_list_stamplead_bank_one_pairweighed_kernel(
    tc, xt_words, xt_scales, xo_words, xo_scales, w_words, w_scales, w0_words, w0_scales, tb,
    wb_words, wb_scales, so, sp, offs, offs2, offs3, offs4, offs5, offs6, offs7, out,
):
    nc = tc.nc
    with ExitStack() as ctx:
        sb = ctx.enter_context(tc.tile_pool(name="sb", bufs=1))
        table = ctx.enter_context(tc.tile_pool(name="table", bufs=1))
        ps = ctx.enter_context(tc.psum_pool(name="ps", bufs=1))

        def load_list(src, name):
            tile = sb.tile(list(src.shape), U16, name=name)
            nc.sync.dma_start(tile[:], src)
            return tile

        def load_words(src, name):
            tile = sb.tile([P, src.shape[2]], U32, name=name, align_bytes=64)
            nc.sync.dma_start(tile[:].bitcast(I32), src[0].rearrange("p n t -> p (n t)").bitcast(I32))
            return tile

        def zeroed_plane(width, name):
            tile = sb.tile([P, width], U8, name=name, align_bytes=64)
            nc.vector.memset(tile[:].bitcast(I32), 0)
            return tile

        def load_plane(tile, src):
            for q in range(QUADS):
                nc.sync.dma_start(tile[32 * q : 32 * q + 4, :].bitcast(I32), src[0, 4 * q : 4 * q + 4, :].bitcast(I32))

        xo_plane = zeroed_plane(Z, "xo_plane")
        xt_plane = zeroed_plane(T, "xt_plane")
        ww_plane = zeroed_plane(2 * R, "ww_plane")
        wb_plane = zeroed_plane(N, "wb_plane")
        pw = [sb.tile([P, C], F32, name="pw%d" % t) for t in range(PACK)]

        ww_stage = sb.tile([4, QUADS, 2 * R // 4], I32, name="ww_stage")
        for i, src in enumerate((w0_scales, w_scales)):
            nc.sync.dma_start(
                ww_stage[:, :, i * R // 4 : (i + 1) * R // 4],
                src[0].bitcast(I32).rearrange("(q r) c -> r q c", r=4),
            )
        load_plane(xo_plane, xo_scales)
        l2 = load_list(offs2, "l2")
        xo_w = load_words(xo_words, "xo_w")
        l1 = load_list(offs, "l1")
        load_plane(xt_plane, xt_scales)
        w0_w = load_words(w0_words, "w0_w")
        xt_w = sb.tile([P, T], U16, name="xt_w")
        nc.sync.dma_start(xt_w[:].bitcast(I32), xt_words[0].bitcast(I32))
        w_w = load_words(w_words, "w_w")
        tb_rows = tb.rearrange("(p t) x -> p t x", t=PACK)
        tbs = [table.tile([P, X], F32, name="tb%d" % t, offset=t * X * 4) for t in range(PACK)]
        l3 = load_list(offs3, "l3")
        l4 = load_list(offs4, "l4")
        for t in range(PACK):
            nc.sync.dma_start(tbs[t][:], tb_rows[:, t, :])
        l5 = load_list(offs5, "l5")
        wb_w = load_words(wb_words, "wb_w")
        load_plane(wb_plane, wb_scales)
        l6 = load_list(offs6, "l6")
        l7 = load_list(offs7, "l7")
        so_sb = sb.tile([P, N // P], F32, name="so_sb")
        sp_sb = sb.tile([P, N // P], F32, name="sp_sb")
        with nc.allow_non_contiguous_dma(reason="one weight a partition and half"):
            nc.sync.dma_start(so_sb[:], so.rearrange("(h p) o -> p (h o)", p=P))
            nc.sync.dma_start(sp_sb[:], sp.rearrange("(h p) o -> p (h o)", p=P))

        ww_words = ww_plane[:].bitcast(I32)
        for q in range(QUADS):
            nc.vector.tensor_copy(ww_words[32 * q : 32 * q + 4, :], ww_stage[:, q, :])
        ww_dealt = sb.tile([P, 2, PACK, P], U8, name="ww_dealt", align_bytes=64)
        nc.vector.tensor_copy(ww_dealt[:], ww_plane[:].rearrange("p (i m t) -> p i t m", i=2, t=PACK))
        w0_dealt = sb.tile([P, R], U32, name="w0_dealt", align_bytes=64)
        w_dealt = sb.tile([P, R], U32, name="w_dealt", align_bytes=64)
        for dealt, words, lo, hi in ((w0_dealt, w0_w, 0, PACK), (w_dealt, w_w, 0, 1), (w_dealt, w_w, 1, PACK)):
            nc.scalar.copy(
                dealt[:].rearrange("p (t m) -> p m t", t=PACK)[:, :, lo:hi],
                words[:].rearrange("p (m t) -> p m t", t=PACK)[:, :, lo:hi],
            )

        xo_g = sb.tile([P, J], U32, name="xo_g", align_bytes=64)
        xo_gs = sb.tile([P, J], U8, name="xo_gs", align_bytes=64)
        xt_g = sb.tile([P, J], U16, name="xt_g", align_bytes=64)
        xt_gs = sb.tile([P, J], U8, name="xt_gs", align_bytes=64)
        nc.vector.tensor_copy(xo_gs[:], xo_plane[:].indirect(l2[:]))
        nc.vector.tensor_copy(xo_g[:], xo_w[:].indirect(l2[:]))
        nc.vector.tensor_copy(xt_gs[:], xt_plane[:].indirect(l1[:]))
        nc.vector.tensor_copy(xt_g[:], xt_w[:].indirect(l1[:]))

        for t in range(PACK):
            nc.vector.memset(pw[t][:], 0.0)

        a_ps = [ps.tile([P, J], F32, name="a_ps%d" % t) for t in range(PACK)]
        for t in range(PACK):
            nc.tensor.matmul_mx(
                out=a_ps[t][:], lhsT=w0_dealt[:, t * P : (t + 1) * P].bitcast(E4M3), lhsT_scale=ww_dealt[:, 0, t, :],
                rhs=xo_g[:].bitcast(E5M2), rhs_scale=xo_gs[:], start=True, stop=False,
            )
        for t in range(PACK):
            nc.tensor.matmul_mx(
                out=a_ps[t][:], lhsT=w_dealt[:, t * P : (t + 1) * P].bitcast(E5M2), lhsT_scale=ww_dealt[:, 1, t, :],
                rhs=xt_g[:].bitcast(E2M1), rhs_scale=xt_gs[:], start=False, stop=True,
            )

        a_sb = [sb.tile([P, J], F32, name="a_sb%d" % t) for t in range(PACK)]
        fetched = [sb.tile([P, C], F32, name="fetched%d" % t) for t in range(PACK)]
        diff = [sb.tile([P, C], F32, name="diff%d" % t, tag="diff%d" % t) for t in range(PACK)]
        pg = {}
        hid_rows = sb.tile([P, PACK, O], BF16, name="hid_rows")
        hid = sb.tile([P, O, PACK], BF16, name="hid", align_bytes=64)

        def empty(t):
            nc.vector.tensor_copy(a_sb[t][:], a_ps[t][:])

        def empty_s(t):
            nc.scalar.copy(a_sb[t][:], a_ps[t][:])

        def sub_g(t):
            nc.gpsimd.tensor_tensor(diff[t][:], pw[t][:], fetched[t][:], ALU.subtract)

        def fetch(t):
            nc.scalar.activation(fetched[t][:], tbs[t][:].indirect(l4[:]), ACT.Copy, scale=a_sb[t][:, 0:1])

        def place_v(t):
            nc.vector.tensor_copy(pw[t][:].indirect(l3[:]), a_sb[t][:])

        def place_s(t):
            nc.scalar.activation(pw[t][:].indirect(l3[:]), a_sb[t][:], ACT.Copy)

        def sub(t):
            nc.vector.tensor_tensor(diff[t][:], pw[t][:], fetched[t][:], ALU.subtract)

        def mag(t):
            if t == PACK - 1:
                pg[t] = sb.tile([P, C], F32, name="pg%d" % t)
            else:
                pg[t] = table.tile([P, C], F32, name="pg%d" % t, offset=(2 * X * 4, 3 * X * 4, 3 * X * 4 + C * 4)[t])
            nc.scalar.activation(pg[t][:], diff[t][:], ACT.Abs)

        def mag_v(t):
            pg[t] = sb.tile([P, C], F32, name="pg%d" % t)
            nc.vector.scalar_tensor_tensor(pg[t][:], diff[t][:], -1.0, diff[t][:], ALU.mult, ALU.max)

        def pick_v(t):
            nc.vector.tensor_copy(hid_rows[:, t, :], pg[t][:].indirect(l5[:]))

        def pick_s(t):
            nc.scalar.activation(hid_rows[:, t, :], pg[t][:].indirect(l5[:]), ACT.Copy)

        def weave(t0):
            nc.vector.tensor_copy(hid[:, :, t0 : t0 + 2], hid_rows[:, t0 : t0 + 2, :].rearrange("p t o -> p o t"))

        empty(0)
        empty(1)
        fetch(0)
        place_v(0)
        empty_s(2)
        sub_g(0)
        fetch(1)
        place_v(1)
        empty_s(3)
        sub_g(1)
        fetch(2)
        place_v(2)
        sub_g(2)
        fetch(3)
        place_v(3)
        sub(3)
        for t in range(PACK):
            mag(t)
        pick_v(0)
        pick_v(1)
        pick_s(2)
        weave(0)
        H = O // 2
        nc.scalar.activation(hid_rows[:, 3, 0:H], pg[3][:].indirect(l5[:, 0 : H // 16]), ACT.Copy)
        nc.vector.tensor_copy(hid_rows[:, 3, H:O], pg[3][:].indirect(l5[:, H // 16 : O // 16]))
        hid_q = sb.tile([P, O], U32, name="hid_q", align_bytes=64)
        hid_s = sb.tile([P, O], U8, name="hid_s", align_bytes=64)
        for j in range(2):
            nc.vector.tensor_copy(
                hid[:, j * H : (j + 1) * H, 2:4], hid_rows[:, 2:4, j * H : (j + 1) * H].rearrange("p t o -> p o t")
            )
        for j in range(2):
            nc.vector.quantize_mx(
                out=hid_q[:, j * H : (j + 1) * H].bitcast(E5M2), scales=hid_s[:, j * H : (j + 1) * H],
                in_=hid[:, j * H : (j + 1) * H, :].rearrange("p o t -> p (o t)"),
            )
        p_sbs = [sb.tile([P, O], F32, name="p_sb%d" % h) for h in range(N // P)]
        for j in range(2):
            for h in range(N // P):
                p_ps = ps.tile([P, H], F32, name="p_ps%d_%d" % (h, j))
                nc.tensor.matmul_mx(
                    out=p_ps[:], lhsT=wb_w[:, h * P : (h + 1) * P].bitcast(E4M3),
                    lhsT_scale=wb_plane[:, h * P : (h + 1) * P],
                    rhs=hid_q[:, j * H : (j + 1) * H].bitcast(E5M2), rhs_scale=hid_s[:, j * H : (j + 1) * H],
                    start=True, stop=True,
                )
                if j == 0:
                    nc.scalar.copy(p_sbs[h][:, j * H : (j + 1) * H], p_ps[:])
                else:
                    nc.vector.tensor_copy(p_sbs[h][:, j * H : (j + 1) * H], p_ps[:])

        for h in range(N // P):
            p_sb = p_sbs[h]
            first = sb.tile([P, U], F32, name="first%d" % h)
            second = sb.tile([P, U], F32, name="second%d" % h)
            nc.scalar.activation(first[:], p_sb[:].indirect(l6[:]), ACT.Copy, scale=so_sb[:, h : h + 1])
            nc.scalar.activation(second[:], p_sb[:].indirect(l7[:]), ACT.Copy, scale=sp_sb[:, h : h + 1])
            y = sb.tile([P, U], F32, name="y%d" % h)
            nc.vector.tensor_tensor(y[:], first[:], second[:], ALU.max)
            nc.sync.dma_start(out[h * P : (h + 1) * P, :], y[:])
